import numpy as np
import ml_dtypes


def mxq(x, axis, fmt="e4m3"):
    dtype, down = {"e4m3": (ml_dtypes.float8_e4m3fn, 7), "e5m2": (ml_dtypes.float8_e5m2, 14)}[fmt]
    v = np.moveaxis(np.asarray(x, np.float32).astype(ml_dtypes.bfloat16).astype(np.float64), axis, -1)
    blocks = v.reshape(v.shape[:-1] + (-1, 32))
    amax = np.abs(blocks).max(-1, keepdims=True)
    byte = np.maximum(np.where(amax > 0, np.frexp(amax)[1] - 1 + 127, 0) - down, 1)
    scale = np.exp2(byte - 127.0)
    codes = (blocks / scale).astype(np.float32).astype(dtype).astype(np.float64)
    return np.moveaxis((codes * scale).reshape(v.shape), -1, axis)


WIDE = False


def mx_kscale(k):
    if not WIDE:
        return np.ones(k)
    levels = np.array([10, -10, 5, -5, 0])
    if k % 512:
        return np.exp2(np.random.permutation(np.resize(levels, k // 32))).repeat(32)
    a = np.empty((k // 512, 16))
    for p in range(k // 512):
        a[p, :8] = np.random.permutation(np.resize(levels, 8))
        for g in range(8):
            far = levels[np.abs(levels - a[p, g]) >= 10]
            a[p, g + 8] = far[np.random.randint(len(far))]
    return np.exp2(a.ravel()).repeat(32)


def f64(x):
    return np.asarray(x).astype(np.float64)


def striped(idx):
    return np.tile(idx.reshape(-1, 16).T, (8, 1)).astype(np.uint16)


def unstriped(offs):
    return offs[:16].T.reshape(-1).astype(np.int64)


def striped8(idx):
    return np.concatenate([x.reshape(-1, 16).T for x in idx]).astype(np.uint16)


def runs(offs, k):
    lists = np.stack([offs[16 * r : 16 * r + 16].T.reshape(-1) for r in range(8)]).astype(np.int64)
    return lists[np.arange(k) % 512 // 64]


def pack_weight(w):
    k, n = w.shape
    w = f64(np.asarray(w, np.float32).astype(ml_dtypes.bfloat16)).reshape(k // 32, 32, n)
    amax = np.abs(w).max(1)
    byte = np.clip(np.where(amax > 0, np.frexp(amax)[1] - 1 + 127 - 7, 1), 1, 254)
    scaled = (w * np.exp2(127.0 - byte)[:, None, :]).reshape(k, n).astype(np.float32)
    words = np.ascontiguousarray(scaled.reshape(k // 512, 128, 4, n).transpose(0, 1, 3, 2)).astype(ml_dtypes.float8_e4m3fn).view(np.uint8)
    return words, np.ascontiguousarray(byte.astype(np.uint8).reshape(k // 512, 16, n))


def unpack_weight(words, scales):
    g, p, n, _ = words.shape
    vals = np.ascontiguousarray(words).view(ml_dtypes.float8_e4m3fn).astype(np.float64) * np.repeat(np.exp2(scales.astype(np.float64) - 127.0), 8, axis=1)[..., None]
    return vals.transpose(0, 1, 3, 2).reshape(g * 512, n)


E2M1 = np.array([0.0, 0.5, 1.0, 1.5, 2.0, 3.0, 4.0, 6.0, -0.0, -0.5, -1.0, -1.5, -2.0, -3.0, -4.0, -6.0])


def pack_fp4(w):
    k, n = w.shape
    w = f64(np.asarray(w, np.float32).astype(ml_dtypes.bfloat16)).reshape(k // 32, 32, n)
    amax = np.abs(w).max(1)
    mant, ex = np.frexp(amax / 6.0)
    byte = np.clip(np.where(amax > 0, np.where(mant > 0.5, ex, ex - 1) + 127, 1), 1, 254)
    scaled = (w * np.exp2(127.0 - byte)[:, None, :]).reshape(k, n).astype(np.float32)
    c = np.ascontiguousarray(scaled.reshape(k // 512, 128, 4, n).transpose(0, 1, 3, 2)).astype(ml_dtypes.float4_e2m1fn).view(np.uint8) & 0xF
    words = (c[..., 0::2] | (c[..., 1::2] << 4)).reshape(k // 512, 128, 2 * n)
    return np.ascontiguousarray(words), np.ascontiguousarray(byte.astype(np.uint8).reshape(k // 512, 16, n))


def unpack_fp4(words, scales):
    g, _, n = scales.shape
    words = np.ascontiguousarray(words).reshape(g, 128, n, 2)
    nib = np.empty((g, 128, n, 4), np.uint8)
    nib[..., 0::2] = words & 0xF
    nib[..., 1::2] = words >> 4
    vals = E2M1[nib] * np.repeat(np.exp2(scales.astype(np.float64) - 127.0), 8, axis=1)[..., None]
    return vals.transpose(0, 1, 3, 2).reshape(g * 512, n)


def sigmoid(v):
    return 1.0 / (1.0 + np.exp(-np.maximum(v, -700.0)))

def planes(y):
    n, m = y.shape
    v = y.astype(np.float32).astype(ml_dtypes.bfloat16).astype(np.float64).reshape(n // 32, 32, m)
    top = np.abs(v).max(1)
    byte = np.clip(np.where(top > 0, np.frexp(top)[1] - 1 + 127 - 7, 1), 1, 254)
    codes = (v * np.exp2(127.0 - byte)[:, None, :]).reshape(n, m).astype(np.float32).astype(ml_dtypes.float8_e4m3fn).view(np.uint8)
    words = codes.reshape(n // 512, 128, 4, m).transpose(0, 1, 3, 2)
    return np.ascontiguousarray(words), np.ascontiguousarray(byte.astype(np.uint8).reshape(n // 512, 16, m))


K, T, S, H, C, W = 512, 2048, 512, 512, 512, 256


def setup_inputs():
    n = np.random.standard_normal
    s = mx_kscale(K)[:, None]
    packed_xT = pack_weight(n((K, T)) * s)
    packed_w1 = pack_fp4(n((K, H)) / np.sqrt(K) / s)
    perm = np.stack([np.random.permutation(S) for _ in range(8)])
    return {
        "x_words": packed_xT[0],
        "x_scales": packed_xT[1],
        "w1_words": packed_w1[0],
        "w1_scales": packed_w1[1],
        "gs": (np.random.uniform(0.5, 1.5, (K, 1)) / s).astype(np.float32),
        "offs": striped(np.random.permutation(T)[:S]),
        "n1": striped8(np.stack([np.random.permutation(S) for _ in range(8)])),
        "n2": striped8(np.stack([np.random.permutation(S) for _ in range(8)])),
        "cand": striped(np.random.permutation(T)[:C]),
        "n3": striped8(perm[:, :W]),
        "n4": striped8(perm[:, W:]),
    }


def reference(x_words, x_scales, w1_words, w1_scales, gs, offs, n1, n2, cand, n3, n4):
    x_cand = unpack_weight(x_words, x_scales)[:, unstriped(cand)]
    xq = unpack_weight(x_words, x_scales)[:, unstriped(offs)]
    y = unpack_fp4(w1_words, w1_scales).T @ xq
    st = y * (sigmoid(y[np.arange(H)[:, None], runs(n1, H)]))
    z = f64(gs) * (st - (st[np.arange(H)[:, None], runs(n2, H)]))
    s = 0.0625 * ((x_cand.T @ mxq(z, 0, "e4m3")))
    pa = s[np.arange(C)[:, None], runs(n3, C)]
    pb = s[np.arange(C)[:, None], runs(n4, C)]
    rb = np.maximum(pa, pb)
    ra = pa / (np.abs(pb) + 0.5)
    ds = np.zeros((C, S))
    ds[np.arange(C)[:, None], runs(n3, C)] = ra
    out = ds.copy()
    out[np.arange(C)[:, None], runs(n4, C)] = rb
    return (out,) + planes(out)

@@ -1,0 +1,189 @@
+from contextlib import ExitStack
+
+import concourse.mybir as mybir
+
+F32 = mybir.dt.float32
+BF16 = mybir.dt.bfloat16
+I32 = mybir.dt.int32
+U32 = mybir.dt.uint32
+U16 = mybir.dt.uint16
+U8 = mybir.dt.uint8
+FP8X4 = mybir.dt.float8_e4m3fn_x4
+FP4X4 = mybir.dt.float4_e2m1fn_x4
+ALU = mybir.AluOpType
+ACT = mybir.ActivationFunctionType
+
+P = 128
+PACK = 4
+T = 2048
+S = 512
+HALF = S // 2
+QUADS = 4
+FLOPS = 2 * 2 * 512 * 512 * 512
+
+
+def tile_picked_candhopgratio_none_po_kernel(
+    tc, x_words, x_scales, w1_words, w1_scales, gs, offs, n1, n2, cand, n3, n4, out_0, out_1, out_2
+):
+    nc = tc.nc
+    with ExitStack() as ctx:
+        lists = ctx.enter_context(tc.tile_pool(name="lists", bufs=1))
+        keep = ctx.enter_context(tc.tile_pool(name="keep", bufs=1))
+        psum = ctx.enter_context(tc.psum_pool(name="psum", bufs=1))
+
+        def load_list(src, name):
+            dst = lists.tile(list(src.shape), U16, name=name)
+            nc.sync.dma_start(dst[:], src)
+            return dst
+
+        def load_scales(queue, dst, src, q):
+            queue.dma_start(dst[32 * q : 32 * q + 4, :].bitcast(I32), src[0, 4 * q : 4 * q + 4, :].bitcast(I32))
+
+        xs = keep.tile([P, T], U8, name="xs", align_bytes=64)
+        ws = keep.tile([P, S], U8, name="ws", align_bytes=64)
+        nc.vector.memset(xs[:].bitcast(I32), 0)
+        nc.gpsimd.memset(ws[:].bitcast(I32), 0)
+        load_scales(nc.gpsimd, ws, w1_scales, QUADS - 1)
+        half = keep.tile([P, 1], F32, name="half")
+        nc.gpsimd.memset(half[:], 0.5)
+
+        offs_sb = load_list(offs, "offs_sb")
+        ww = keep.tile([P, 2 * S], U8, name="ww", align_bytes=64)
+        nc.sync.dma_start(ww[:].bitcast(I32), w1_words[0].bitcast(I32))
+        cand_sb = load_list(cand, "cand_sb")
+        xw = keep.tile([P, T], I32, name="xw", align_bytes=64)
+        nc.sync.dma_start(xw[:], x_words[0].rearrange("p n t -> p (n t)").bitcast(I32))
+        for q in range(QUADS):
+            load_scales(nc.sync, xs, x_scales, q)
+        for q in range(QUADS - 1):
+            load_scales(nc.sync, ws, w1_scales, q)
+        n1_sb = load_list(n1, "n1_sb")
+        gs_sb = keep.tile([P, PACK], F32, name="gs_sb")
+        nc.sync.dma_start(gs_sb[:], gs.rearrange("(p t) o -> p (t o)", t=PACK))
+        n2_sb = load_list(n2, "n2_sb")
+        n4_sb = load_list(n4, "n4_sb")
+        n3_sb = load_list(n3, "n3_sb")
+
+        xq_s = keep.tile([P, S], U8, name="xq_s", align_bytes=64)
+        nc.vector.tensor_copy(xq_s[:], xs[:].indirect(offs_sb[:]))
+        wd = keep.tile([P, 2 * S], U8, name="wd", align_bytes=64)
+        nc.vector.tensor_copy(
+            wd[:].rearrange("p (t m b) -> p m t b", t=PACK, b=2), ww[:].rearrange("p (m t b) -> p m t b", t=PACK, b=2)
+        )
+        wsd = keep.tile([P, S], U8, name="wsd", align_bytes=64)
+        nc.vector.tensor_copy(
+            wsd[:].rearrange("p (t m) -> p m t", t=PACK), ws[:].rearrange("p (m t) -> p m t", t=PACK)
+        )
+        xq_w = keep.tile([P, S], I32, name="xq_w", align_bytes=64)
+        nc.vector.tensor_copy(xq_w[:].bitcast(U32), xw[:].bitcast(U32).indirect(offs_sb[:]))
+
+        y_ps = [psum.tile([P, S], F32, name="y_ps%d" % t, tag="bank%d" % t) for t in range(PACK)]
+        for t in range(PACK):
+            nc.tensor.matmul_mx(
+                out=y_ps[t][:],
+                lhsT=wd[:, 2 * P * t : 2 * P * (t + 1)].bitcast(FP4X4),
+                lhsT_scale=wsd[:, P * t : P * (t + 1)],
+                rhs=xq_w[:].bitcast(FP8X4),
+                rhs_scale=xq_s[:],
+                start=True,
+                stop=True,
+            )
+
+        xc_w = keep.tile([P, S], I32, name="xc_w", align_bytes=64)
+        nc.vector.tensor_copy(
+            xc_w[:].bitcast(U32).rearrange("p (t m) -> p m t", t=PACK), xw[:].bitcast(U32).indirect(cand_sb[:])
+        )
+        xc_s_list = keep.tile([P, S], U8, name="xc_s_list", align_bytes=64)
+        nc.vector.tensor_copy(xc_s_list[:], xs[:].indirect(cand_sb[:]))
+        xc_s = keep.tile([P, S], U8, name="xc_s", align_bytes=64)
+        nc.vector.tensor_copy(
+            xc_s[:].rearrange("p (t m) -> p m t", t=PACK), xc_s_list[:].rearrange("p (m t) -> p m t", t=PACK)
+        )
+
+        halves = [(slice(h * HALF, (h + 1) * HALF), slice(h * HALF // 16, (h + 1) * HALF // 16)) for h in range(2)]
+        low, high = halves[0][0], halves[1][0]
+        neg_z = keep.tile([P, PACK, S], F32, name="neg_z")
+        zb = keep.tile([P, S, PACK], BF16, name="zb", align_bytes=64)
+        for pair in range(2):
+            tiles = (2 * pair, 2 * pair + 1)
+            st = {}
+            st_plain = {}
+            for t in tiles:
+                y = keep.tile([P, S], F32, name="y%d" % t)
+                nc.scalar.copy(y[:], y_ps[t][:])
+                sig = keep.tile([P, S], F32, name="sig%d" % t)
+                for cols, entries in halves:
+                    nc.scalar.activation(sig[:, cols], y[:].indirect(n1_sb[:, entries]), ACT.Sigmoid)
+                st[t] = keep.tile([P, S], F32, name="st%d" % t)
+                nc.vector.scalar_tensor_tensor(st[t][:], y_ps[t][:], gs_sb[:, t : t + 1], sig[:], ALU.mult, ALU.mult)
+            for t in tiles:
+                st_plain[t] = keep.tile([P, S], F32, name="st_plain%d" % t)
+                nc.vector.tensor_copy(st_plain[t][:], st[t][:])
+            for t in tiles:
+                for cols, entries in halves:
+                    nc.vector.tensor_tensor(
+                        neg_z[:, t, cols], st[t][:].indirect(n2_sb[:, entries]), st_plain[t][:, cols], ALU.subtract
+                    )
+        nc.scalar.activation(zb[:, :, 0:2], neg_z[:, 0:2, :].rearrange("p t j -> p j t"), ACT.Copy, scale=-1.0)
+        nc.scalar.activation(zb[:, low, 2:4], neg_z[:, 2:4, low].rearrange("p t j -> p j t"), ACT.Copy, scale=-1.0)
+        nc.vector.tensor_scalar(zb[:, high, 2:4], neg_z[:, 2:4, high].rearrange("p t j -> p j t"), -1.0, None, ALU.mult)
+        zq_w = keep.tile([P, S], I32, name="zq_w", align_bytes=64)
+        zq_s = keep.tile([P, S], U8, name="zq_s", align_bytes=64)
+        for cols in (high, low):
+            nc.vector.quantize_mx(
+                out=zq_w[:, cols].bitcast(FP8X4), scales=zq_s[:, cols], in_=zb[:, cols, :].rearrange("p j t -> p (j t)")
+            )
+
+        pa = keep.tile([P, PACK, HALF], F32, name="pa")
+        pb = keep.tile([P, PACK, HALF], F32, name="pb")
+        size = keep.tile([P, PACK, HALF], F32, name="size")
+        bank = PACK
+        for t in range(PACK):
+            s = keep.tile([P, S], F32, name="s%d" % t)
+            for cols in (high, low) if t == 0 else (slice(0, S),):
+                s_ps = psum.tile([P, cols.stop - cols.start], F32, name="s_ps", tag="bank%d" % (bank % 8))
+                bank = bank + 1
+                nc.tensor.matmul_mx(
+                    out=s_ps[:],
+                    lhsT=xc_w[:, P * t : P * (t + 1)].bitcast(FP8X4),
+                    lhsT_scale=xc_s[:, P * t : P * (t + 1)],
+                    rhs=zq_w[:, cols].bitcast(FP8X4),
+                    rhs_scale=zq_s[:, cols],
+                    start=True,
+                    stop=True,
+                )
+                nc.scalar.activation(s[:, cols], s_ps[:], ACT.Copy, scale=0.0625)
+            nc.vector.tensor_copy(pb[:, t, :], s[:].indirect(n4_sb[:]))
+            nc.vector.tensor_copy(pa[:, t, :], s[:].indirect(n3_sb[:]))
+            nc.scalar.activation(size[:, t, :], pb[:, t, :], ACT.Abs)
+        log_size = keep.tile([P, PACK, HALF], F32, name="log_size")
+        nc.scalar.activation(log_size[:], size[:], ACT.Ln, bias=half[:])
+        recip = keep.tile([P, PACK, HALF], F32, name="recip")
+        nc.scalar.activation(recip[:], log_size[:], ACT.Exp, scale=-1.0)
+        rb = keep.tile([P, PACK, HALF], F32, name="rb")
+        nc.vector.tensor_tensor(rb[:], pa[:], pb[:], ALU.max)
+
+        out_rows = out_0.rearrange("(p t) j -> p t j", t=PACK)
+        ob = keep.tile([P, S, PACK], BF16, name="ob", align_bytes=64)
+        res = [keep.tile([P, S], F32, name="o%d" % t) for t in range(PACK)]
+        for t in range(PACK):
+            nc.vector.tensor_copy(res[t][:].indirect(n4_sb[:]), rb[:, t, :])
+        for t in range(PACK):
+            nc.vector.tensor_tensor(res[t][:].indirect(n3_sb[:]), pa[:, t, :], recip[:, t, :], ALU.mult)
+            nc.sync.dma_start(out_rows[:, t, :], res[t][:])
+            if t < 2:
+                nc.scalar.copy(ob[:, :, t], res[t][:])
+            else:
+                nc.scalar.copy(ob[:, low, t], res[t][:, low])
+                nc.vector.tensor_copy(ob[:, high, t], res[t][:, high])
+        oq_w = keep.tile([P, S], I32, name="oq_w", align_bytes=64)
+        oq_s = keep.tile([P, S], U8, name="oq_s", align_bytes=64)
+        words_out = out_1[0].rearrange("p n t -> p (n t)").bitcast(I32)
+        for cols in (high, low):
+            nc.vector.quantize_mx(
+                out=oq_w[:, cols].bitcast(FP8X4), scales=oq_s[:, cols], in_=ob[:, cols, :].rearrange("p j t -> p (j t)")
+            )
+            nc.sync.dma_start(words_out[:, cols], oq_w[:, cols])
+        for q in range(QUADS):
+            queue = nc.sync if q % 2 else nc.scalar
+            queue.dma_start(out_2[0, 4 * q : 4 * q + 4, :].bitcast(I32), oq_s[32 * q : 32 * q + 4, :].bitcast(I32))

@@ -41,21 +41,23 @@ def tile_picked_candhopgratio_none_po_kernel(
 
         xs = keep.tile([P, T], U8, name="xs", align_bytes=64)
         ws = keep.tile([P, S], U8, name="ws", align_bytes=64)
-        nc.vector.memset(xs[:].bitcast(I32), 0)
+        nc.vector.memset(xs[:, : T // 2].bitcast(I32), 0)
+        nc.gpsimd.memset(xs[:, T // 2 :].bitcast(I32), 0)
         nc.gpsimd.memset(ws[:].bitcast(I32), 0)
-        load_scales(nc.gpsimd, ws, w1_scales, QUADS - 1)
+        zero = keep.tile([P, 1], F32, name="zero")
+        nc.vector.memset(zero[:], 0.0)
         half = keep.tile([P, 1], F32, name="half")
-        nc.gpsimd.memset(half[:], 0.5)
+        nc.scalar.activation(half[:], zero[:], ACT.Sigmoid)
 
-        offs_sb = load_list(offs, "offs_sb")
         ww = keep.tile([P, 2 * S], U8, name="ww", align_bytes=64)
         nc.sync.dma_start(ww[:].bitcast(I32), w1_words[0].bitcast(I32))
+        offs_sb = load_list(offs, "offs_sb")
         cand_sb = load_list(cand, "cand_sb")
+        for q in range(QUADS):
+            load_scales(nc.sync, xs, x_scales, q)
         xw = keep.tile([P, T], I32, name="xw", align_bytes=64)
         nc.sync.dma_start(xw[:], x_words[0].rearrange("p n t -> p (n t)").bitcast(I32))
         for q in range(QUADS):
-            load_scales(nc.sync, xs, x_scales, q)
-        for q in range(QUADS - 1):
             load_scales(nc.sync, ws, w1_scales, q)
         n1_sb = load_list(n1, "n1_sb")
         gs_sb = keep.tile([P, PACK], F32, name="gs_sb")
@@ -64,30 +66,37 @@ def tile_picked_candhopgratio_none_po_kernel(
         n4_sb = load_list(n4, "n4_sb")
         n3_sb = load_list(n3, "n3_sb")
 
+        halves = [(slice(h * HALF, (h + 1) * HALF), slice(h * HALF // 16, (h + 1) * HALF // 16)) for h in range(2)]
+        low, high = halves[0][0], halves[1][0]
+        whole = slice(0, S)
         xq_s = keep.tile([P, S], U8, name="xq_s", align_bytes=64)
         nc.vector.tensor_copy(xq_s[:], xs[:].indirect(offs_sb[:]))
         wd = keep.tile([P, 2 * S], U8, name="wd", align_bytes=64)
-        nc.vector.tensor_copy(
-            wd[:].rearrange("p (t m b) -> p m t b", t=PACK, b=2), ww[:].rearrange("p (m t b) -> p m t b", t=PACK, b=2)
+        nc.gpsimd.tensor_copy(
+            wd[:].rearrange("p (t m b) -> p t m b", t=PACK, b=2), ww[:].rearrange("p (m t b) -> p t m b", t=PACK, b=2)
         )
         wsd = keep.tile([P, S], U8, name="wsd", align_bytes=64)
-        nc.vector.tensor_copy(
-            wsd[:].rearrange("p (t m) -> p m t", t=PACK), ws[:].rearrange("p (m t) -> p m t", t=PACK)
+        nc.gpsimd.tensor_copy(
+            wsd[:].rearrange("p (t m) -> p t m", t=PACK), ws[:].rearrange("p (m t) -> p t m", t=PACK)
         )
         xq_w = keep.tile([P, S], I32, name="xq_w", align_bytes=64)
-        nc.vector.tensor_copy(xq_w[:].bitcast(U32), xw[:].bitcast(U32).indirect(offs_sb[:]))
+        for cols, entries in halves:
+            nc.vector.tensor_copy(xq_w[:, cols].bitcast(U32), xw[:].bitcast(U32).indirect(offs_sb[:, entries]))
 
-        y_ps = [psum.tile([P, S], F32, name="y_ps%d" % t, tag="bank%d" % t) for t in range(PACK)]
-        for t in range(PACK):
+        pieces = [(0, low), (0, high)] + [(t, whole) for t in range(1, PACK)]
+        y_ps = []
+        for bank, (t, cols) in enumerate(pieces):
+            acc = psum.tile([P, cols.stop - cols.start], F32, name="y_ps", tag="bank%d" % bank)
             nc.tensor.matmul_mx(
-                out=y_ps[t][:],
+                out=acc[:],
                 lhsT=wd[:, 2 * P * t : 2 * P * (t + 1)].bitcast(FP4X4),
                 lhsT_scale=wsd[:, P * t : P * (t + 1)],
-                rhs=xq_w[:].bitcast(FP8X4),
-                rhs_scale=xq_s[:],
+                rhs=xq_w[:, cols].bitcast(FP8X4),
+                rhs_scale=xq_s[:, cols],
                 start=True,
                 stop=True,
             )
+            y_ps.append((t, cols, acc))
 
         xc_w = keep.tile([P, S], I32, name="xc_w", align_bytes=64)
         nc.vector.tensor_copy(
@@ -100,36 +109,58 @@ def tile_picked_candhopgratio_none_po_kernel(
             xc_s[:].rearrange("p (t m) -> p m t", t=PACK), xc_s_list[:].rearrange("p (m t) -> p m t", t=PACK)
         )
 
-        halves = [(slice(h * HALF, (h + 1) * HALF), slice(h * HALF // 16, (h + 1) * HALF // 16)) for h in range(2)]
-        low, high = halves[0][0], halves[1][0]
         neg_z = keep.tile([P, PACK, S], F32, name="neg_z")
         zb = keep.tile([P, S, PACK], BF16, name="zb", align_bytes=64)
-        for pair in range(2):
-            tiles = (2 * pair, 2 * pair + 1)
-            st = {}
-            st_plain = {}
-            for t in tiles:
-                y = keep.tile([P, S], F32, name="y%d" % t)
-                nc.scalar.copy(y[:], y_ps[t][:])
-                sig = keep.tile([P, S], F32, name="sig%d" % t)
-                for cols, entries in halves:
-                    nc.scalar.activation(sig[:, cols], y[:].indirect(n1_sb[:, entries]), ACT.Sigmoid)
-                st[t] = keep.tile([P, S], F32, name="st%d" % t)
-                nc.vector.scalar_tensor_tensor(st[t][:], y_ps[t][:], gs_sb[:, t : t + 1], sig[:], ALU.mult, ALU.mult)
-            for t in tiles:
-                st_plain[t] = keep.tile([P, S], F32, name="st_plain%d" % t)
-                nc.vector.tensor_copy(st_plain[t][:], st[t][:])
-            for t in tiles:
-                for cols, entries in halves:
-                    nc.vector.tensor_tensor(
-                        neg_z[:, t, cols], st[t][:].indirect(n2_sb[:, entries]), st_plain[t][:, cols], ALU.subtract
-                    )
-        nc.scalar.activation(zb[:, :, 0:2], neg_z[:, 0:2, :].rearrange("p t j -> p j t"), ACT.Copy, scale=-1.0)
+
+        def empty(t):
+            y = keep.tile([P, S], F32, name="y%d" % t)
+            for tile_no, cols, acc in y_ps:
+                if tile_no == t and t in (1, 2):
+                    nc.vector.tensor_copy(y[:, cols], acc[:])
+                elif tile_no == t:
+                    nc.scalar.copy(y[:, cols], acc[:])
+            return y
+
+        ys = [empty(t) for t in range(3)]
+
+        def gate(t):
+            y = ys[t] if t < 3 else empty(t)
+            sig = keep.tile([P, S], F32, name="sig%d" % t)
+            for cols, entries in halves:
+                nc.scalar.activation(sig[:, cols], y[:].indirect(n1_sb[:, entries]), ACT.Sigmoid)
+            st = keep.tile([P, S], F32, name="st%d" % t)
+            nc.vector.scalar_tensor_tensor(st[:], y[:], gs_sb[:, t : t + 1], sig[:], ALU.mult, ALU.mult)
+            return st
+
+        def hop(t, h):
+            cols, entries = halves[h]
+            nc.vector.tensor_tensor(
+                neg_z[:, t, cols], st[t][:].indirect(n2_sb[:, entries]), st_plain[:, t, cols], ALU.subtract
+            )
+
+        st_plain = keep.tile([P, PACK, S], F32, name="st_plain")
+        st = [gate(0)]
+        nc.vector.tensor_copy(st_plain[:, 0, :], st[0][:])
+        st.append(gate(1))
+        hop(0, 0)
+        nc.vector.tensor_copy(st_plain[:, 1, :], st[1][:])
+        hop(0, 1)
+        st.append(gate(2))
+        hop(1, 0)
+        hop(1, 1)
+        st.append(gate(3))
+        nc.scalar.copy(st_plain[:, 2, :], st[2][:])
+        nc.scalar.copy(st_plain[:, 3, :], st[3][:])
+        for t in (2, 3):
+            hop(t, 0)
+            hop(t, 1)
+        for cols in (low, high):
+            nc.scalar.activation(zb[:, cols, 0:2], neg_z[:, 0:2, cols].rearrange("p t j -> p j t"), ACT.Copy, scale=-1.0)
         nc.scalar.activation(zb[:, low, 2:4], neg_z[:, 2:4, low].rearrange("p t j -> p j t"), ACT.Copy, scale=-1.0)
         nc.vector.tensor_scalar(zb[:, high, 2:4], neg_z[:, 2:4, high].rearrange("p t j -> p j t"), -1.0, None, ALU.mult)
         zq_w = keep.tile([P, S], I32, name="zq_w", align_bytes=64)
         zq_s = keep.tile([P, S], U8, name="zq_s", align_bytes=64)
-        for cols in (high, low):
+        for cols in (low, high):
             nc.vector.quantize_mx(
                 out=zq_w[:, cols].bitcast(FP8X4), scales=zq_s[:, cols], in_=zb[:, cols, :].rearrange("p j t -> p (j t)")
             )
@@ -137,10 +168,10 @@ def tile_picked_candhopgratio_none_po_kernel(
         pa = keep.tile([P, PACK, HALF], F32, name="pa")
         pb = keep.tile([P, PACK, HALF], F32, name="pb")
         size = keep.tile([P, PACK, HALF], F32, name="size")
-        bank = PACK
+        bank = len(pieces)
         for t in range(PACK):
             s = keep.tile([P, S], F32, name="s%d" % t)
-            for cols in (high, low) if t == 0 else (slice(0, S),):
+            for cols in (low, high) if t == 0 else (whole,):
                 s_ps = psum.tile([P, cols.stop - cols.start], F32, name="s_ps", tag="bank%d" % (bank % 8))
                 bank = bank + 1
                 nc.tensor.matmul_mx(

@@ -75,7 +75,7 @@ def tile_picked_candhopgratio_none_po_kernel(
         nc.gpsimd.tensor_copy(
             wd[:].rearrange("p (t m b) -> p t m b", t=PACK, b=2), ww[:].rearrange("p (m t b) -> p t m b", t=PACK, b=2)
         )
-        wsd = keep.tile([P, S], U8, name="wsd", align_bytes=64)
+        wsd = keep.tile([P, S], U8, name="wsd", tag="stationary_scales", align_bytes=64)
         nc.gpsimd.tensor_copy(
             wsd[:].rearrange("p (t m) -> p t m", t=PACK), ws[:].rearrange("p (m t) -> p t m", t=PACK)
         )
@@ -83,9 +83,7 @@ def tile_picked_candhopgratio_none_po_kernel(
         for cols, entries in halves:
             nc.vector.tensor_copy(xq_w[:, cols].bitcast(U32), xw[:].bitcast(U32).indirect(offs_sb[:, entries]))
 
-        pieces = [(0, low), (0, high)] + [(t, whole) for t in range(1, PACK)]
-        y_ps = []
-        for bank, (t, cols) in enumerate(pieces):
+        def project(t, cols, bank):
             acc = psum.tile([P, cols.stop - cols.start], F32, name="y_ps", tag="bank%d" % bank)
             nc.tensor.matmul_mx(
                 out=acc[:],
@@ -96,7 +94,12 @@ def tile_picked_candhopgratio_none_po_kernel(
                 start=True,
                 stop=True,
             )
-            y_ps.append((t, cols, acc))
+            return acc
+
+        ys = [keep.tile([P, S], F32, name="y%d" % t) for t in range(PACK)]
+        for bank, cols in enumerate((low, high)):
+            nc.scalar.copy(ys[0][:, cols], project(0, cols, bank)[:])
+        y_ps = {1: project(1, whole, 2)}
 
         xc_w = keep.tile([P, S], I32, name="xc_w", align_bytes=64)
         nc.vector.tensor_copy(
@@ -104,7 +107,10 @@ def tile_picked_candhopgratio_none_po_kernel(
         )
         xc_s_list = keep.tile([P, S], U8, name="xc_s_list", align_bytes=64)
         nc.vector.tensor_copy(xc_s_list[:], xs[:].indirect(cand_sb[:]))
-        xc_s = keep.tile([P, S], U8, name="xc_s", align_bytes=64)
+        nc.vector.tensor_copy(ys[1][:], y_ps[1][:])
+        y_ps[2] = project(2, whole, 1)
+        y_ps[3] = project(3, whole, 2)
+        xc_s = keep.tile([P, S], U8, name="xc_s", tag="stationary_scales", align_bytes=64)
         nc.vector.tensor_copy(
             xc_s[:].rearrange("p (t m) -> p m t", t=PACK), xc_s_list[:].rearrange("p (m t) -> p m t", t=PACK)
         )
@@ -112,19 +118,10 @@ def tile_picked_candhopgratio_none_po_kernel(
         neg_z = keep.tile([P, PACK, S], F32, name="neg_z")
         zb = keep.tile([P, S, PACK], BF16, name="zb", align_bytes=64)
 
-        def empty(t):
-            y = keep.tile([P, S], F32, name="y%d" % t)
-            for tile_no, cols, acc in y_ps:
-                if tile_no == t and t in (1, 2):
-                    nc.vector.tensor_copy(y[:, cols], acc[:])
-                elif tile_no == t:
-                    nc.scalar.copy(y[:, cols], acc[:])
-            return y
-
-        ys = [empty(t) for t in range(3)]
-
         def gate(t):
-            y = ys[t] if t < 3 else empty(t)
+            y = ys[t]
+            if t >= 2:
+                nc.scalar.copy(y[:], y_ps[t][:])
             sig = keep.tile([P, S], F32, name="sig%d" % t)
             for cols, entries in halves:
                 nc.scalar.activation(sig[:, cols], y[:].indirect(n1_sb[:, entries]), ACT.Sigmoid)
@@ -132,8 +129,8 @@ def tile_picked_candhopgratio_none_po_kernel(
             nc.vector.scalar_tensor_tensor(st[:], y[:], gs_sb[:, t : t + 1], sig[:], ALU.mult, ALU.mult)
             return st
 
-        def hop(t, h):
-            cols, entries = halves[h]
+        def hop(t, cols):
+            entries = slice(cols.start // 16, cols.stop // 16)
             nc.vector.tensor_tensor(
                 neg_z[:, t, cols], st[t][:].indirect(n2_sb[:, entries]), st_plain[:, t, cols], ALU.subtract
             )
@@ -142,22 +139,25 @@ def tile_picked_candhopgratio_none_po_kernel(
         st = [gate(0)]
         nc.vector.tensor_copy(st_plain[:, 0, :], st[0][:])
         st.append(gate(1))
-        hop(0, 0)
+        hop(0, low)
         nc.vector.tensor_copy(st_plain[:, 1, :], st[1][:])
-        hop(0, 1)
+        hop(0, high)
         st.append(gate(2))
-        hop(1, 0)
-        hop(1, 1)
+        hop(1, low)
+        hop(1, high)
         st.append(gate(3))
         nc.scalar.copy(st_plain[:, 2, :], st[2][:])
         nc.scalar.copy(st_plain[:, 3, :], st[3][:])
-        for t in (2, 3):
-            hop(t, 0)
-            hop(t, 1)
+        last_quarters = (slice(HALF, HALF + HALF // 2), slice(HALF + HALF // 2, S))
+        for t, cols in ((2, low), (2, high), (3, low), (3, last_quarters[0]), (3, last_quarters[1])):
+            hop(t, cols)
         for cols in (low, high):
             nc.scalar.activation(zb[:, cols, 0:2], neg_z[:, 0:2, cols].rearrange("p t j -> p j t"), ACT.Copy, scale=-1.0)
         nc.scalar.activation(zb[:, low, 2:4], neg_z[:, 2:4, low].rearrange("p t j -> p j t"), ACT.Copy, scale=-1.0)
-        nc.vector.tensor_scalar(zb[:, high, 2:4], neg_z[:, 2:4, high].rearrange("p t j -> p j t"), -1.0, None, ALU.mult)
+        for cols in last_quarters:
+            nc.vector.tensor_scalar(
+                zb[:, cols, 2:4], neg_z[:, 2:4, cols].rearrange("p t j -> p j t"), -1.0, None, ALU.mult
+            )
         zq_w = keep.tile([P, S], I32, name="zq_w", align_bytes=64)
         zq_s = keep.tile([P, S], U8, name="zq_s", align_bytes=64)
         for cols in (low, high):
@@ -168,7 +168,7 @@ def tile_picked_candhopgratio_none_po_kernel(
         pa = keep.tile([P, PACK, HALF], F32, name="pa")
         pb = keep.tile([P, PACK, HALF], F32, name="pb")
         size = keep.tile([P, PACK, HALF], F32, name="size")
-        bank = len(pieces)
+        bank = 3
         for t in range(PACK):
             s = keep.tile([P, S], F32, name="s%d" % t)
             for cols in (low, high) if t == 0 else (whole,):

@@ -17,9 +17,20 @@ P = 128
 PACK = 4
 T = 2048
 S = 512
-HALF = S // 2
+PAIRS = S // 2
 QUADS = 4
-FLOPS = 2 * 2 * 512 * 512 * 512
+BANKS = 8
+FLOPS = 2 * 2 * S * S * S
+
+WHOLE = slice(0, S)
+LOW, HIGH = slice(0, S // 2), slice(S // 2, S)
+LAST_QUARTERS = (slice(S // 2, 3 * S // 4), slice(3 * S // 4, S))
+ALL_PAIRS = slice(0, PAIRS)
+LOW_PAIRS, HIGH_PAIRS = slice(0, PAIRS // 2), slice(PAIRS // 2, PAIRS)
+
+
+def entries(list_tile, cols):
+    return list_tile[:, cols.start // 16 : cols.stop // 16]
 
 
 def tile_picked_candhopgratio_none_po_kernel(
@@ -36,11 +47,32 @@ def tile_picked_candhopgratio_none_po_kernel(
             nc.sync.dma_start(dst[:], src)
             return dst
 
-        def load_scales(queue, dst, src, q):
-            queue.dma_start(dst[32 * q : 32 * q + 4, :].bitcast(I32), src[0, 4 * q : 4 * q + 4, :].bitcast(I32))
+        def load_scales(dst, src):
+            for q in range(QUADS):
+                nc.sync.dma_start(dst[32 * q : 32 * q + 4, :].bitcast(I32), src[0, 4 * q : 4 * q + 4, :].bitcast(I32))
+
+        def mx_product(stationary, stationary_scales, moving, moving_scales, bank):
+            acc = psum.tile([P, moving_scales.shape[1]], F32, name="acc", tag="bank%d" % bank)
+            nc.tensor.matmul_mx(
+                out=acc[:],
+                lhsT=stationary,
+                lhsT_scale=stationary_scales,
+                rhs=moving.bitcast(FP8X4),
+                rhs_scale=moving_scales,
+                start=True,
+                stop=True,
+            )
+            return acc
+
+        def quantize(words, scales, rounded, cols):
+            nc.vector.quantize_mx(
+                out=words[:, cols].bitcast(FP8X4),
+                scales=scales[:, cols],
+                in_=rounded[:, cols, :].rearrange("p j t -> p (j t)"),
+            )
 
         xs = keep.tile([P, T], U8, name="xs", align_bytes=64)
-        ws = keep.tile([P, S], U8, name="ws", align_bytes=64)
+        ws = keep.tile([P, S], U8, name="ws", tag="raw_scales", align_bytes=64)
         nc.vector.memset(xs[:, : T // 2].bitcast(I32), 0)
         nc.gpsimd.memset(xs[:, T // 2 :].bitcast(I32), 0)
         nc.gpsimd.memset(ws[:].bitcast(I32), 0)
@@ -53,12 +85,10 @@ def tile_picked_candhopgratio_none_po_kernel(
         nc.sync.dma_start(ww[:].bitcast(I32), w1_words[0].bitcast(I32))
         offs_sb = load_list(offs, "offs_sb")
         cand_sb = load_list(cand, "cand_sb")
-        for q in range(QUADS):
-            load_scales(nc.sync, xs, x_scales, q)
+        load_scales(xs, x_scales)
         xw = keep.tile([P, T], I32, name="xw", align_bytes=64)
         nc.sync.dma_start(xw[:], x_words[0].rearrange("p n t -> p (n t)").bitcast(I32))
-        for q in range(QUADS):
-            load_scales(nc.sync, ws, w1_scales, q)
+        load_scales(ws, w1_scales)
         n1_sb = load_list(n1, "n1_sb")
         gs_sb = keep.tile([P, PACK], F32, name="gs_sb")
         nc.sync.dma_start(gs_sb[:], gs.rearrange("(p t) o -> p (t o)", t=PACK))
@@ -66,9 +96,6 @@ def tile_picked_candhopgratio_none_po_kernel(
         n4_sb = load_list(n4, "n4_sb")
         n3_sb = load_list(n3, "n3_sb")
 
-        halves = [(slice(h * HALF, (h + 1) * HALF), slice(h * HALF // 16, (h + 1) * HALF // 16)) for h in range(2)]
-        low, high = halves[0][0], halves[1][0]
-        whole = slice(0, S)
         xq_s = keep.tile([P, S], U8, name="xq_s", align_bytes=64)
         nc.vector.tensor_copy(xq_s[:], xs[:].indirect(offs_sb[:]))
         wd = keep.tile([P, 2 * S], U8, name="wd", align_bytes=64)
@@ -80,140 +107,143 @@ def tile_picked_candhopgratio_none_po_kernel(
             wsd[:].rearrange("p (t m) -> p t m", t=PACK), ws[:].rearrange("p (m t) -> p t m", t=PACK)
         )
         xq_w = keep.tile([P, S], I32, name="xq_w", align_bytes=64)
-        for cols, entries in halves:
-            nc.vector.tensor_copy(xq_w[:, cols].bitcast(U32), xw[:].bitcast(U32).indirect(offs_sb[:, entries]))
+        for cols in (LOW, HIGH):
+            nc.vector.tensor_copy(xq_w[:, cols].bitcast(U32), xw[:].bitcast(U32).indirect(entries(offs_sb, cols)))
 
         def project(t, cols, bank):
-            acc = psum.tile([P, cols.stop - cols.start], F32, name="y_ps", tag="bank%d" % bank)
-            nc.tensor.matmul_mx(
-                out=acc[:],
-                lhsT=wd[:, 2 * P * t : 2 * P * (t + 1)].bitcast(FP4X4),
-                lhsT_scale=wsd[:, P * t : P * (t + 1)],
-                rhs=xq_w[:, cols].bitcast(FP8X4),
-                rhs_scale=xq_s[:, cols],
-                start=True,
-                stop=True,
+            return mx_product(
+                wd[:, 2 * P * t : 2 * P * (t + 1)].bitcast(FP4X4),
+                wsd[:, P * t : P * (t + 1)],
+                xq_w[:, cols],
+                xq_s[:, cols],
+                bank,
             )
-            return acc
 
         ys = [keep.tile([P, S], F32, name="y%d" % t) for t in range(PACK)]
-        for bank, cols in enumerate((low, high)):
+        for bank, cols in enumerate((LOW, HIGH)):
             nc.scalar.copy(ys[0][:, cols], project(0, cols, bank)[:])
-        y_ps = {1: project(1, whole, 2)}
+        y_ps = {1: project(1, WHOLE, 2)}
 
         xc_w = keep.tile([P, S], I32, name="xc_w", align_bytes=64)
         nc.vector.tensor_copy(
             xc_w[:].bitcast(U32).rearrange("p (t m) -> p m t", t=PACK), xw[:].bitcast(U32).indirect(cand_sb[:])
         )
-        xc_s_list = keep.tile([P, S], U8, name="xc_s_list", align_bytes=64)
-        nc.vector.tensor_copy(xc_s_list[:], xs[:].indirect(cand_sb[:]))
+        xc_s_listed = []
+        for cols, tag in ((LOW, "cand_scales"), (HIGH, "raw_scales")):
+            part = keep.tile([P, S // 2], U8, name="xc_s_listed", tag=tag, align_bytes=64)
+            nc.vector.tensor_copy(part[:], xs[:].indirect(entries(cand_sb, cols)))
+            xc_s_listed.append(part)
         nc.vector.tensor_copy(ys[1][:], y_ps[1][:])
-        y_ps[2] = project(2, whole, 1)
-        y_ps[3] = project(3, whole, 2)
+        y_ps[2] = project(2, WHOLE, 1)
+        y_ps[3] = project(3, WHOLE, 2)
         xc_s = keep.tile([P, S], U8, name="xc_s", tag="stationary_scales", align_bytes=64)
-        nc.vector.tensor_copy(
-            xc_s[:].rearrange("p (t m) -> p m t", t=PACK), xc_s_list[:].rearrange("p (m t) -> p m t", t=PACK)
-        )
+        for h, part in enumerate(xc_s_listed):
+            nc.vector.tensor_copy(
+                xc_s[:].rearrange("p (t m) -> p m t", t=PACK)[:, h * P // 2 : (h + 1) * P // 2, :],
+                part[:].rearrange("p (m t) -> p m t", t=PACK),
+            )
 
         neg_z = keep.tile([P, PACK, S], F32, name="neg_z")
         zb = keep.tile([P, S, PACK], BF16, name="zb", align_bytes=64)
 
         def gate(t):
-            y = ys[t]
             if t >= 2:
-                nc.scalar.copy(y[:], y_ps[t][:])
+                nc.scalar.copy(ys[t][:], y_ps[t][:])
             sig = keep.tile([P, S], F32, name="sig%d" % t)
-            for cols, entries in halves:
-                nc.scalar.activation(sig[:, cols], y[:].indirect(n1_sb[:, entries]), ACT.Sigmoid)
-            st = keep.tile([P, S], F32, name="st%d" % t)
-            nc.vector.scalar_tensor_tensor(st[:], y[:], gs_sb[:, t : t + 1], sig[:], ALU.mult, ALU.mult)
-            return st
+            for cols in (LOW, HIGH):
+                nc.scalar.activation(sig[:, cols], ys[t][:].indirect(entries(n1_sb, cols)), ACT.Sigmoid)
+            weighted = keep.tile([P, S], F32, name="st%d" % t)
+            for cols in (LOW, HIGH) if t == 0 else (WHOLE,):
+                nc.vector.scalar_tensor_tensor(
+                    weighted[:, cols], ys[t][:, cols], gs_sb[:, t : t + 1], sig[:, cols], ALU.mult, ALU.mult
+                )
+            return weighted
 
         def hop(t, cols):
-            entries = slice(cols.start // 16, cols.stop // 16)
             nc.vector.tensor_tensor(
-                neg_z[:, t, cols], st[t][:].indirect(n2_sb[:, entries]), st_plain[:, t, cols], ALU.subtract
+                neg_z[:, t, cols], st[t][:].indirect(entries(n2_sb, cols)), st_plain[:, t, cols], ALU.subtract
             )
 
         st_plain = keep.tile([P, PACK, S], F32, name="st_plain")
         st = [gate(0)]
-        nc.vector.tensor_copy(st_plain[:, 0, :], st[0][:])
+        for cols in (LOW, HIGH):
+            nc.vector.tensor_copy(st_plain[:, 0, cols], st[0][:, cols])
         st.append(gate(1))
-        hop(0, low)
+        hop(0, LOW)
         nc.vector.tensor_copy(st_plain[:, 1, :], st[1][:])
-        hop(0, high)
+        hop(0, HIGH)
         st.append(gate(2))
-        hop(1, low)
-        hop(1, high)
+        hop(1, LOW)
+        hop(1, HIGH)
         st.append(gate(3))
-        nc.scalar.copy(st_plain[:, 2, :], st[2][:])
-        nc.scalar.copy(st_plain[:, 3, :], st[3][:])
-        last_quarters = (slice(HALF, HALF + HALF // 2), slice(HALF + HALF // 2, S))
-        for t, cols in ((2, low), (2, high), (3, low), (3, last_quarters[0]), (3, last_quarters[1])):
-            hop(t, cols)
-        for cols in (low, high):
-            nc.scalar.activation(zb[:, cols, 0:2], neg_z[:, 0:2, cols].rearrange("p t j -> p j t"), ACT.Copy, scale=-1.0)
-        nc.scalar.activation(zb[:, low, 2:4], neg_z[:, 2:4, low].rearrange("p t j -> p j t"), ACT.Copy, scale=-1.0)
-        for cols in last_quarters:
+        for t in (2, 3):
+            nc.scalar.copy(st_plain[:, t, :], st[t][:])
+        for cols in (LOW, HIGH):
+            hop(2, cols)
+        for cols in (LOW,) + LAST_QUARTERS:
+            hop(3, cols)
+
+        for cols, pair in ((LOW, slice(0, 2)), (HIGH, slice(0, 2)), (LOW, slice(2, 4))):
+            nc.scalar.activation(
+                zb[:, cols, pair], neg_z[:, pair, cols].rearrange("p t j -> p j t"), ACT.Copy, scale=-1.0
+            )
+        for cols in LAST_QUARTERS:
             nc.vector.tensor_scalar(
                 zb[:, cols, 2:4], neg_z[:, 2:4, cols].rearrange("p t j -> p j t"), -1.0, None, ALU.mult
             )
         zq_w = keep.tile([P, S], I32, name="zq_w", align_bytes=64)
         zq_s = keep.tile([P, S], U8, name="zq_s", align_bytes=64)
-        for cols in (low, high):
-            nc.vector.quantize_mx(
-                out=zq_w[:, cols].bitcast(FP8X4), scales=zq_s[:, cols], in_=zb[:, cols, :].rearrange("p j t -> p (j t)")
-            )
+        for cols in (LOW,) + LAST_QUARTERS:
+            quantize(zq_w, zq_s, zb, cols)
 
-        pa = keep.tile([P, PACK, HALF], F32, name="pa")
-        pb = keep.tile([P, PACK, HALF], F32, name="pb")
-        size = keep.tile([P, PACK, HALF], F32, name="size")
+        pa = keep.tile([P, PACK, PAIRS], F32, name="pa")
+        pb = keep.tile([P, PACK, PAIRS], F32, name="pb")
+        size = keep.tile([P, PACK, PAIRS], F32, name="size")
         bank = 3
         for t in range(PACK):
             s = keep.tile([P, S], F32, name="s%d" % t)
-            for cols in (low, high) if t == 0 else (whole,):
-                s_ps = psum.tile([P, cols.stop - cols.start], F32, name="s_ps", tag="bank%d" % (bank % 8))
-                bank = bank + 1
-                nc.tensor.matmul_mx(
-                    out=s_ps[:],
-                    lhsT=xc_w[:, P * t : P * (t + 1)].bitcast(FP8X4),
-                    lhsT_scale=xc_s[:, P * t : P * (t + 1)],
-                    rhs=zq_w[:, cols].bitcast(FP8X4),
-                    rhs_scale=zq_s[:, cols],
-                    start=True,
-                    stop=True,
+            for cols in (LOW,) + LAST_QUARTERS if t == 0 else (WHOLE,):
+                acc = mx_product(
+                    xc_w[:, P * t : P * (t + 1)].bitcast(FP8X4),
+                    xc_s[:, P * t : P * (t + 1)],
+                    zq_w[:, cols],
+                    zq_s[:, cols],
+                    bank % BANKS,
                 )
-                nc.scalar.activation(s[:, cols], s_ps[:], ACT.Copy, scale=0.0625)
+                bank = bank + 1
+                nc.scalar.activation(s[:, cols], acc[:], ACT.Copy, scale=0.0625)
             nc.vector.tensor_copy(pb[:, t, :], s[:].indirect(n4_sb[:]))
-            nc.vector.tensor_copy(pa[:, t, :], s[:].indirect(n3_sb[:]))
+            for cols in (LOW_PAIRS, HIGH_PAIRS) if t == PACK - 1 else (ALL_PAIRS,):
+                nc.vector.tensor_copy(pa[:, t, cols], s[:].indirect(entries(n3_sb, cols)))
             nc.scalar.activation(size[:, t, :], pb[:, t, :], ACT.Abs)
-        log_size = keep.tile([P, PACK, HALF], F32, name="log_size")
+
+        log_size = keep.tile([P, PACK, PAIRS], F32, name="log_size")
         nc.scalar.activation(log_size[:], size[:], ACT.Ln, bias=half[:])
-        recip = keep.tile([P, PACK, HALF], F32, name="recip")
+        recip = keep.tile([P, PACK, PAIRS], F32, name="recip")
         nc.scalar.activation(recip[:], log_size[:], ACT.Exp, scale=-1.0)
-        rb = keep.tile([P, PACK, HALF], F32, name="rb")
-        nc.vector.tensor_tensor(rb[:], pa[:], pb[:], ALU.max)
+        rb = keep.tile([P, PACK, PAIRS], F32, name="rb")
+        for cols in (LOW_PAIRS, HIGH_PAIRS):
+            nc.vector.tensor_tensor(rb[:, :, cols], pa[:, :, cols], pb[:, :, cols], ALU.max)
 
         out_rows = out_0.rearrange("(p t) j -> p t j", t=PACK)
         ob = keep.tile([P, S, PACK], BF16, name="ob", align_bytes=64)
-        res = [keep.tile([P, S], F32, name="o%d" % t) for t in range(PACK)]
-        for t in range(PACK):
-            nc.vector.tensor_copy(res[t][:].indirect(n4_sb[:]), rb[:, t, :])
+        res = [keep.tile([P, S], F32, name="res%d" % t) for t in range(PACK)]
+        for t, cols in ((0, LOW_PAIRS), (1, ALL_PAIRS), (0, HIGH_PAIRS), (2, ALL_PAIRS), (3, ALL_PAIRS)):
+            nc.vector.tensor_copy(res[t][:].indirect(entries(n4_sb, cols)), rb[:, t, cols])
         for t in range(PACK):
             nc.vector.tensor_tensor(res[t][:].indirect(n3_sb[:]), pa[:, t, :], recip[:, t, :], ALU.mult)
             nc.sync.dma_start(out_rows[:, t, :], res[t][:])
             if t < 2:
                 nc.scalar.copy(ob[:, :, t], res[t][:])
             else:
-                nc.scalar.copy(ob[:, low, t], res[t][:, low])
-                nc.vector.tensor_copy(ob[:, high, t], res[t][:, high])
+                nc.scalar.copy(ob[:, LOW, t], res[t][:, LOW])
+                nc.vector.tensor_copy(ob[:, HIGH, t], res[t][:, HIGH])
+
         oq_w = keep.tile([P, S], I32, name="oq_w", align_bytes=64)
         oq_s = keep.tile([P, S], U8, name="oq_s", align_bytes=64)
         words_out = out_1[0].rearrange("p n t -> p (n t)").bitcast(I32)
-        for cols in (high, low):
-            nc.vector.quantize_mx(
-                out=oq_w[:, cols].bitcast(FP8X4), scales=oq_s[:, cols], in_=ob[:, cols, :].rearrange("p j t -> p (j t)")
-            )
+        for cols in (HIGH, LOW):
+            quantize(oq_w, oq_s, ob, cols)
             nc.sync.dma_start(words_out[:, cols], oq_w[:, cols])
         for q in range(QUADS):
             queue = nc.sync if q % 2 else nc.scalar

@@ -76,10 +76,8 @@ def tile_picked_candhopgratio_none_po_kernel(
         nc.vector.memset(xs[:, : T // 2].bitcast(I32), 0)
         nc.gpsimd.memset(xs[:, T // 2 :].bitcast(I32), 0)
         nc.gpsimd.memset(ws[:].bitcast(I32), 0)
-        zero = keep.tile([P, 1], F32, name="zero")
-        nc.vector.memset(zero[:], 0.0)
         half = keep.tile([P, 1], F32, name="half")
-        nc.scalar.activation(half[:], zero[:], ACT.Sigmoid)
+        nc.gpsimd.memset(half[:], 0.5)
 
         ww = keep.tile([P, 2 * S], U8, name="ww", align_bytes=64)
         nc.sync.dma_start(ww[:].bitcast(I32), w1_words[0].bitcast(I32))
@@ -120,8 +118,12 @@ def tile_picked_candhopgratio_none_po_kernel(
             )
 
         ys = [keep.tile([P, S], F32, name="y%d" % t) for t in range(PACK)]
-        for bank, cols in enumerate((LOW, HIGH)):
-            nc.scalar.copy(ys[0][:, cols], project(0, cols, bank)[:])
+        first = [project(0, cols, bank) for bank, cols in enumerate((LOW, HIGH))]
+        sig_first = keep.tile([P, S], F32, name="sig_first")
+        for acc, cols in zip(first, (LOW, HIGH)):
+            nc.scalar.activation(sig_first[:, cols], acc[:], ACT.Sigmoid)
+        for acc, cols in zip(first, (LOW, HIGH)):
+            nc.scalar.activation(ys[0][:, cols], acc[:], ACT.Copy, scale=gs_sb[:, 0:1])
         y_ps = {1: project(1, WHOLE, 2)}
 
         xc_w = keep.tile([P, S], I32, name="xc_w", align_bytes=64)
@@ -133,7 +135,7 @@ def tile_picked_candhopgratio_none_po_kernel(
             part = keep.tile([P, S // 2], U8, name="xc_s_listed", tag=tag, align_bytes=64)
             nc.vector.tensor_copy(part[:], xs[:].indirect(entries(cand_sb, cols)))
             xc_s_listed.append(part)
-        nc.vector.tensor_copy(ys[1][:], y_ps[1][:])
+        nc.scalar.copy(ys[1][:], y_ps[1][:])
         y_ps[2] = project(2, WHOLE, 1)
         y_ps[3] = project(3, WHOLE, 2)
         xc_s = keep.tile([P, S], U8, name="xc_s", tag="stationary_scales", align_bytes=64)
@@ -153,10 +155,7 @@ def tile_picked_candhopgratio_none_po_kernel(
             for cols in (LOW, HIGH):
                 nc.scalar.activation(sig[:, cols], ys[t][:].indirect(entries(n1_sb, cols)), ACT.Sigmoid)
             weighted = keep.tile([P, S], F32, name="st%d" % t)
-            for cols in (LOW, HIGH) if t == 0 else (WHOLE,):
-                nc.vector.scalar_tensor_tensor(
-                    weighted[:, cols], ys[t][:, cols], gs_sb[:, t : t + 1], sig[:, cols], ALU.mult, ALU.mult
-                )
+            nc.vector.scalar_tensor_tensor(weighted[:], ys[t][:], gs_sb[:, t : t + 1], sig[:], ALU.mult, ALU.mult)
             return weighted
 
         def hop(t, cols):
@@ -165,7 +164,11 @@ def tile_picked_candhopgratio_none_po_kernel(
             )
 
         st_plain = keep.tile([P, PACK, S], F32, name="st_plain")
-        st = [gate(0)]
+        st = [keep.tile([P, S], F32, name="st0")]
+        for cols in (LOW, HIGH):
+            nc.vector.tensor_tensor(
+                st[0][:, cols], sig_first[:].indirect(entries(n1_sb, cols)), ys[0][:, cols], ALU.mult
+            )
         for cols in (LOW, HIGH):
             nc.vector.tensor_copy(st_plain[:, 0, cols], st[0][:, cols])
         st.append(gate(1))

from contextlib import ExitStack

import concourse.mybir as mybir

F32 = mybir.dt.float32
BF16 = mybir.dt.bfloat16
I32 = mybir.dt.int32
U32 = mybir.dt.uint32
U16 = mybir.dt.uint16
U8 = mybir.dt.uint8
FP8X4 = mybir.dt.float8_e4m3fn_x4
FP4X4 = mybir.dt.float4_e2m1fn_x4
ALU = mybir.AluOpType
ACT = mybir.ActivationFunctionType

P = 128
PACK = 4
T = 2048
S = 512
PAIRS = S // 2
QUADS = 4
BANKS = 8
FLOPS = 2 * 2 * S * S * S

WHOLE = slice(0, S)
LOW, HIGH = slice(0, S // 2), slice(S // 2, S)
LAST_QUARTERS = (slice(S // 2, 3 * S // 4), slice(3 * S // 4, S))
ALL_PAIRS = slice(0, PAIRS)
LOW_PAIRS, HIGH_PAIRS = slice(0, PAIRS // 2), slice(PAIRS // 2, PAIRS)


def entries(list_tile, cols):
    return list_tile[:, cols.start // 16 : cols.stop // 16]


def tile_picked_candhopgratio_none_po_kernel(
    tc, x_words, x_scales, w1_words, w1_scales, gs, offs, n1, n2, cand, n3, n4, out_0, out_1, out_2
):
    nc = tc.nc
    with ExitStack() as ctx:
        lists = ctx.enter_context(tc.tile_pool(name="lists", bufs=1))
        keep = ctx.enter_context(tc.tile_pool(name="keep", bufs=1))
        psum = ctx.enter_context(tc.psum_pool(name="psum", bufs=1))

        def load_list(src, name):
            dst = lists.tile(list(src.shape), U16, name=name)
            nc.sync.dma_start(dst[:], src)
            return dst

        def load_scales(dst, src):
            for q in range(QUADS):
                nc.sync.dma_start(dst[32 * q : 32 * q + 4, :].bitcast(I32), src[0, 4 * q : 4 * q + 4, :].bitcast(I32))

        def mx_product(stationary, stationary_scales, moving, moving_scales, bank):
            acc = psum.tile([P, moving_scales.shape[1]], F32, name="acc", tag="bank%d" % bank)
            nc.tensor.matmul_mx(
                out=acc[:],
                lhsT=stationary,
                lhsT_scale=stationary_scales,
                rhs=moving.bitcast(FP8X4),
                rhs_scale=moving_scales,
                start=True,
                stop=True,
            )
            return acc

        def quantize(words, scales, rounded, cols):
            nc.vector.quantize_mx(
                out=words[:, cols].bitcast(FP8X4),
                scales=scales[:, cols],
                in_=rounded[:, cols, :].rearrange("p j t -> p (j t)"),
            )

        xs = keep.tile([P, T], U8, name="xs", align_bytes=64)
        ws = keep.tile([P, S], U8, name="ws", tag="raw_scales", align_bytes=64)
        nc.vector.memset(xs[:, : T // 2].bitcast(I32), 0)
        nc.gpsimd.memset(xs[:, T // 2 :].bitcast(I32), 0)
        nc.gpsimd.memset(ws[:].bitcast(I32), 0)
        half = keep.tile([P, 1], F32, name="half")
        nc.gpsimd.memset(half[:], 0.5)

        ww = keep.tile([P, 2 * S], U8, name="ww", align_bytes=64)
        nc.sync.dma_start(ww[:].bitcast(I32), w1_words[0].bitcast(I32))
        offs_sb = load_list(offs, "offs_sb")
        cand_sb = load_list(cand, "cand_sb")
        load_scales(xs, x_scales)
        xw = keep.tile([P, T], I32, name="xw", align_bytes=64)
        nc.sync.dma_start(xw[:], x_words[0].rearrange("p n t -> p (n t)").bitcast(I32))
        load_scales(ws, w1_scales)
        n1_sb = load_list(n1, "n1_sb")
        gs_sb = keep.tile([P, PACK], F32, name="gs_sb")
        nc.sync.dma_start(gs_sb[:], gs.rearrange("(p t) o -> p (t o)", t=PACK))
        n2_sb = load_list(n2, "n2_sb")
        n4_sb = load_list(n4, "n4_sb")
        n3_sb = load_list(n3, "n3_sb")

        xq_s = keep.tile([P, S], U8, name="xq_s", align_bytes=64)
        nc.vector.tensor_copy(xq_s[:], xs[:].indirect(offs_sb[:]))
        wd = keep.tile([P, 2 * S], U8, name="wd", align_bytes=64)
        nc.gpsimd.tensor_copy(
            wd[:].rearrange("p (t m b) -> p t m b", t=PACK, b=2), ww[:].rearrange("p (m t b) -> p t m b", t=PACK, b=2)
        )
        wsd = keep.tile([P, S], U8, name="wsd", tag="stationary_scales", align_bytes=64)
        nc.gpsimd.tensor_copy(
            wsd[:].rearrange("p (t m) -> p t m", t=PACK), ws[:].rearrange("p (m t) -> p t m", t=PACK)
        )
        xq_w = keep.tile([P, S], I32, name="xq_w", align_bytes=64)
        for cols in (LOW, HIGH):
            nc.vector.tensor_copy(xq_w[:, cols].bitcast(U32), xw[:].bitcast(U32).indirect(entries(offs_sb, cols)))

        def project(t, cols, bank):
            return mx_product(
                wd[:, 2 * P * t : 2 * P * (t + 1)].bitcast(FP4X4),
                wsd[:, P * t : P * (t + 1)],
                xq_w[:, cols],
                xq_s[:, cols],
                bank,
            )

        ys = [keep.tile([P, S], F32, name="y%d" % t) for t in range(PACK)]
        first = [project(0, cols, bank) for bank, cols in enumerate((LOW, HIGH))]
        sig_first = keep.tile([P, S], F32, name="sig_first")
        for acc, cols in zip(first, (LOW, HIGH)):
            nc.scalar.activation(sig_first[:, cols], acc[:], ACT.Sigmoid)
        for acc, cols in zip(first, (LOW, HIGH)):
            nc.scalar.activation(ys[0][:, cols], acc[:], ACT.Copy, scale=gs_sb[:, 0:1])
        y_ps = {1: project(1, WHOLE, 2)}

        xc_w = keep.tile([P, S], I32, name="xc_w", align_bytes=64)
        nc.vector.tensor_copy(
            xc_w[:].bitcast(U32).rearrange("p (t m) -> p m t", t=PACK), xw[:].bitcast(U32).indirect(cand_sb[:])
        )
        xc_s_listed = []
        for cols, tag in ((LOW, "cand_scales"), (HIGH, "raw_scales")):
            part = keep.tile([P, S // 2], U8, name="xc_s_listed", tag=tag, align_bytes=64)
            nc.vector.tensor_copy(part[:], xs[:].indirect(entries(cand_sb, cols)))
            xc_s_listed.append(part)
        nc.scalar.copy(ys[1][:], y_ps[1][:])
        y_ps[2] = project(2, WHOLE, 1)
        y_ps[3] = project(3, WHOLE, 2)
        xc_s = keep.tile([P, S], U8, name="xc_s", tag="stationary_scales", align_bytes=64)
        for h, part in enumerate(xc_s_listed):
            nc.vector.tensor_copy(
                xc_s[:].rearrange("p (t m) -> p m t", t=PACK)[:, h * P // 2 : (h + 1) * P // 2, :],
                part[:].rearrange("p (m t) -> p m t", t=PACK),
            )

        neg_z = keep.tile([P, PACK, S], F32, name="neg_z")
        zb = keep.tile([P, S, PACK], BF16, name="zb", align_bytes=64)

        def gate(t):
            if t >= 2:
                nc.scalar.copy(ys[t][:], y_ps[t][:])
            sig = keep.tile([P, S], F32, name="sig%d" % t)
            for cols in (LOW, HIGH):
                nc.scalar.activation(sig[:, cols], ys[t][:].indirect(entries(n1_sb, cols)), ACT.Sigmoid)
            weighted = keep.tile([P, S], F32, name="st%d" % t)
            nc.vector.scalar_tensor_tensor(weighted[:], ys[t][:], gs_sb[:, t : t + 1], sig[:], ALU.mult, ALU.mult)
            return weighted

        def hop(t, cols):
            nc.vector.tensor_tensor(
                neg_z[:, t, cols], st[t][:].indirect(entries(n2_sb, cols)), st_plain[:, t, cols], ALU.subtract
            )

        st_plain = keep.tile([P, PACK, S], F32, name="st_plain")
        st = [keep.tile([P, S], F32, name="st0")]
        for cols in (LOW, HIGH):
            nc.vector.tensor_tensor(
                st[0][:, cols], sig_first[:].indirect(entries(n1_sb, cols)), ys[0][:, cols], ALU.mult
            )
        for cols in (LOW, HIGH):
            nc.vector.tensor_copy(st_plain[:, 0, cols], st[0][:, cols])
        st.append(gate(1))
        hop(0, LOW)
        nc.vector.tensor_copy(st_plain[:, 1, :], st[1][:])
        hop(0, HIGH)
        st.append(gate(2))
        hop(1, LOW)
        hop(1, HIGH)
        st.append(gate(3))
        for t in (2, 3):
            nc.scalar.copy(st_plain[:, t, :], st[t][:])
        for cols in (LOW, HIGH):
            hop(2, cols)
        for cols in (LOW,) + LAST_QUARTERS:
            hop(3, cols)

        for cols, pair in ((LOW, slice(0, 2)), (HIGH, slice(0, 2)), (LOW, slice(2, 4))):
            nc.scalar.activation(
                zb[:, cols, pair], neg_z[:, pair, cols].rearrange("p t j -> p j t"), ACT.Copy, scale=-1.0
            )
        for cols in LAST_QUARTERS:
            nc.vector.tensor_scalar(
                zb[:, cols, 2:4], neg_z[:, 2:4, cols].rearrange("p t j -> p j t"), -1.0, None, ALU.mult
            )
        zq_w = keep.tile([P, S], I32, name="zq_w", align_bytes=64)
        zq_s = keep.tile([P, S], U8, name="zq_s", align_bytes=64)
        for cols in (LOW,) + LAST_QUARTERS:
            quantize(zq_w, zq_s, zb, cols)

        pa = keep.tile([P, PACK, PAIRS], F32, name="pa")
        pb = keep.tile([P, PACK, PAIRS], F32, name="pb")
        size = keep.tile([P, PACK, PAIRS], F32, name="size")
        bank = 3
        for t in range(PACK):
            s = keep.tile([P, S], F32, name="s%d" % t)
            for cols in (LOW,) + LAST_QUARTERS if t == 0 else (WHOLE,):
                acc = mx_product(
                    xc_w[:, P * t : P * (t + 1)].bitcast(FP8X4),
                    xc_s[:, P * t : P * (t + 1)],
                    zq_w[:, cols],
                    zq_s[:, cols],
                    bank % BANKS,
                )
                bank = bank + 1
                nc.scalar.activation(s[:, cols], acc[:], ACT.Copy, scale=0.0625)
            nc.vector.tensor_copy(pb[:, t, :], s[:].indirect(n4_sb[:]))
            for cols in (LOW_PAIRS, HIGH_PAIRS) if t == PACK - 1 else (ALL_PAIRS,):
                nc.vector.tensor_copy(pa[:, t, cols], s[:].indirect(entries(n3_sb, cols)))
            nc.scalar.activation(size[:, t, :], pb[:, t, :], ACT.Abs)

        log_size = keep.tile([P, PACK, PAIRS], F32, name="log_size")
        nc.scalar.activation(log_size[:], size[:], ACT.Ln, bias=half[:])
        recip = keep.tile([P, PACK, PAIRS], F32, name="recip")
        nc.scalar.activation(recip[:], log_size[:], ACT.Exp, scale=-1.0)
        rb = keep.tile([P, PACK, PAIRS], F32, name="rb")
        for cols in (LOW_PAIRS, HIGH_PAIRS):
            nc.vector.tensor_tensor(rb[:, :, cols], pa[:, :, cols], pb[:, :, cols], ALU.max)

        out_rows = out_0.rearrange("(p t) j -> p t j", t=PACK)
        ob = keep.tile([P, S, PACK], BF16, name="ob", align_bytes=64)
        res = [keep.tile([P, S], F32, name="res%d" % t) for t in range(PACK)]
        for t, cols in ((0, LOW_PAIRS), (1, ALL_PAIRS), (0, HIGH_PAIRS), (2, ALL_PAIRS), (3, ALL_PAIRS)):
            nc.vector.tensor_copy(res[t][:].indirect(entries(n4_sb, cols)), rb[:, t, cols])
        for t in range(PACK):
            nc.vector.tensor_tensor(res[t][:].indirect(n3_sb[:]), pa[:, t, :], recip[:, t, :], ALU.mult)
            nc.sync.dma_start(out_rows[:, t, :], res[t][:])
            if t < 2:
                nc.scalar.copy(ob[:, :, t], res[t][:])
            else:
                nc.scalar.copy(ob[:, LOW, t], res[t][:, LOW])
                nc.vector.tensor_copy(ob[:, HIGH, t], res[t][:, HIGH])

        oq_w = keep.tile([P, S], I32, name="oq_w", align_bytes=64)
        oq_s = keep.tile([P, S], U8, name="oq_s", align_bytes=64)
        words_out = out_1[0].rearrange("p n t -> p (n t)").bitcast(I32)
        for cols in (HIGH, LOW):
            quantize(oq_w, oq_s, ob, cols)
            nc.sync.dma_start(words_out[:, cols], oq_w[:, cols])
        for q in range(QUADS):
            queue = nc.sync if q % 2 else nc.scalar
            queue.dma_start(out_2[0, 4 * q : 4 * q + 4, :].bitcast(I32), oq_s[32 * q : 32 * q + 4, :].bitcast(I32))
